import numpy as np
import ml_dtypes


def mxq(x, axis, fmt="e4m3"):
    dtype, down = {"e4m3": (ml_dtypes.float8_e4m3fn, 7), "e5m2": (ml_dtypes.float8_e5m2, 14)}[fmt]
    v = np.moveaxis(np.asarray(x, np.float32).astype(ml_dtypes.bfloat16).astype(np.float64), axis, -1)
    blocks = v.reshape(v.shape[:-1] + (-1, 32))
    amax = np.abs(blocks).max(-1, keepdims=True)
    byte = np.maximum(np.where(amax > 0, np.frexp(amax)[1] - 1 + 127, 0) - down, 1)
    scale = np.exp2(byte - 127.0)
    codes = (blocks / scale).astype(np.float32).astype(dtype).astype(np.float64)
    return np.moveaxis((codes * scale).reshape(v.shape), -1, axis)


WIDE = False


def mx_kscale(k):
    if not WIDE:
        return np.ones(k)
    levels = np.array([10, -10, 5, -5, 0])
    if k % 512:
        return np.exp2(np.random.permutation(np.resize(levels, k // 32))).repeat(32)
    a = np.empty((k // 512, 16))
    for p in range(k // 512):
        a[p, :8] = np.random.permutation(np.resize(levels, 8))
        for g in range(8):
            far = levels[np.abs(levels - a[p, g]) >= 10]
            a[p, g + 8] = far[np.random.randint(len(far))]
    return np.exp2(a.ravel()).repeat(32)


def f64(x):
    return np.asarray(x).astype(np.float64)


def striped8(idx):
    return np.asarray(idx).reshape(8, -1, 16).transpose(0, 2, 1).reshape(128, -1).astype(np.uint16)


def unstriped8(offs):
    return offs.reshape(8, 16, -1).transpose(0, 2, 1).reshape(8, -1).astype(np.int64)


def pick8(x, idx, run):
    r = np.arange(len(x))
    return x[r[:, None], idx[r % (8 * run) // run]]


E2M1 = np.array([0.0, 0.5, 1.0, 1.5, 2.0, 3.0, 4.0, 6.0, -0.0, -0.5, -1.0, -1.5, -2.0, -3.0, -4.0, -6.0])


def pack_weight(w, fmt):
    k, n = w.shape
    w = f64(np.asarray(w, np.float32).astype(ml_dtypes.bfloat16)).reshape(k // 32, 32, n)
    amax = np.abs(w).max(1)
    if fmt == "e4m3":
        byte = np.frexp(amax)[1] - 1 + 127 - 7
    else:
        mant, ex = np.frexp(amax / 6.0)
        byte = np.where(mant > 0.5, ex, ex - 1) + 127
    byte = np.clip(np.where(amax > 0, byte, 1), 1, 254)
    scaled = (w * np.exp2(127.0 - byte)[:, None, :]).reshape(k, n).astype(np.float32)
    by_word = np.ascontiguousarray(scaled.reshape(k // 512, 128, 4, n).transpose(0, 1, 3, 2))
    if fmt == "e4m3":
        words = by_word.astype(ml_dtypes.float8_e4m3fn).view(np.uint8)
    else:
        c = by_word.astype(ml_dtypes.float4_e2m1fn).view(np.uint8) & 0xF
        words = (c[..., 0::2] | (c[..., 1::2] << 4)).reshape(k // 512, 128, 2 * n)
    return np.ascontiguousarray(words), np.ascontiguousarray(byte.astype(np.uint8).reshape(k // 512, 16, n))


def unpack_weight(words, scales, fmt):
    g, _, n = scales.shape
    words = np.ascontiguousarray(words).reshape(g, 128, n, -1)
    if fmt == "e4m3":
        vals = words.view(ml_dtypes.float8_e4m3fn).astype(np.float64)
    else:
        nib = np.empty((g, 128, n, 4), np.uint8)
        nib[..., 0::2] = words & 0xF
        nib[..., 1::2] = words >> 4
        vals = E2M1[nib]
    vals = vals * np.repeat(np.exp2(scales.astype(np.float64) - 127.0), 8, axis=1)[..., None]
    return vals.transpose(0, 1, 3, 2).reshape(g * 512, n)


D, T, I, Q = 512, 1024, 512, 128


def setup_inputs():
    n = np.random.standard_normal
    idx = np.stack([np.random.permutation(T)[:I] for _ in range(8)])
    idx2 = np.stack([np.random.permutation(T)[:I] for _ in range(8)])
    idx3 = np.stack([np.random.permutation(T)[:I] for _ in range(8)])
    fd = mx_kscale(D)
    keysp = pack_weight(n((D, T)) / fd[:, None], "e2m1")
    return {
        "query": (n((D, Q)) * 1.0 / np.sqrt(D) * fd[:, None]).astype(np.float32),
        "query2": (n((D, Q)) * 1.0 / np.sqrt(D) * fd[:, None]).astype(np.float32),
        "keys_words": keysp[0],
        "keys_scales": keysp[1],
        "old": (1.0 * n((Q, T))).astype(np.float32),
        "share2": (np.random.uniform(0.4, 1.2, (Q, 1))).astype(np.float32),
        "offs": striped8(idx),
        "offs2": striped8(idx2),
        "offs3": striped8(idx3),
    }


def reference(query, query2, keys_words, keys_scales, old, share2, offs, offs2, offs3):
    idx = unstriped8(offs)
    idx2 = unstriped8(offs2)
    idx3 = unstriped8(offs3)
    keysu = unpack_weight(keys_words, keys_scales, "e2m1")
    queryq = mxq(f64(query), 0, "e4m3")
    a = queryq.T @ keysu
    query2q = mxq(f64(query2), 0, "e4m3")
    b = query2q.T @ keysu
    s = pick8(a, idx, 16) * pick8(b, idx2, 16)
    p = np.exp(s - np.max(s, axis=1, keepdims=True))
    w = p / np.sum(p, axis=1, keepdims=True)
    ws = w * 256.0
    f1 = np.zeros((Q, T))
    f1[np.arange(Q)[:, None], idx[np.arange(Q) % 128 // 16]] = ws
    f2 = np.zeros((Q, T))
    f2[np.arange(Q)[:, None], idx3[np.arange(Q) % 128 // 16]] = ws
    y = f64(old) + f1 + f2 * f64(share2)
    return y

@@ -1,0 +1,118 @@
+from contextlib import ExitStack
+
+import concourse.mybir as mybir
+
+D, T, I, Q = 512, 1024, 512, 128
+FLOPS = 2 * 2 * D * Q * T
+
+F32 = mybir.dt.float32
+BF16 = mybir.dt.bfloat16
+I32 = mybir.dt.int32
+U32 = mybir.dt.uint32
+U16 = mybir.dt.uint16
+U8 = mybir.dt.uint8
+FP8X4 = mybir.dt.float8_e4m3fn_x4
+FP4X4 = mybir.dt.float4_e2m1fn_x4
+ALU = mybir.AluOpType
+ACT = mybir.ActivationFunctionType
+
+P = 128
+PACK = 4
+N = 256
+HALF = I // 2
+OUT_CHUNK = 256
+
+
+def tile_attend_crossproduct_soft_twiceput_heads_kernel(tc, query, query2, keys_words, keys_scales, old, share2, offs, offs2, offs3, out):
+    nc = tc.nc
+    with ExitStack() as ctx:
+        sb = ctx.enter_context(tc.tile_pool(name="sb", bufs=1))
+        psum = ctx.enter_context(tc.psum_pool(name="psum", bufs=1))
+
+        list1 = sb.tile([P, I // 16], U16, name="list1")
+        list2 = sb.tile([P, I // 16], U16, name="list2")
+        list3 = sb.tile([P, I // 16], U16, name="list3")
+        raw1 = sb.tile([P, PACK, Q], F32, name="raw1")
+        raw2 = sb.tile([P, PACK, Q], F32, name="raw2")
+        key_words = sb.tile([P, 2 * T], U8, name="key_words", align_bytes=64)
+        key_scales = sb.tile([P, T], U8, name="key_scales", align_bytes=64)
+        old_sb = sb.tile([P, T], F32, name="old_sb")
+        share = sb.tile([P, 1], F32, name="share")
+        f1 = sb.tile([P, T], F32, name="f1")
+        f2 = sb.tile([P, T], F32, name="f2")
+
+        nc.vector.memset(key_scales[:].bitcast(I32), 0)
+        nc.sync.dma_start(out=raw1[:], in_=query.rearrange("(p j) q -> p j q", j=PACK))
+        nc.sync.dma_start(out=key_words[:].bitcast(I32), in_=keys_words[0].bitcast(I32))
+        for g in range(4):
+            nc.scalar.dma_start(out=key_scales[32 * g : 32 * g + 4, :].bitcast(I32), in_=keys_scales[0, 4 * g : 4 * g + 4, :].bitcast(I32))
+        nc.sync.dma_start(out=raw2[:], in_=query2.rearrange("(p j) q -> p j q", j=PACK))
+        nc.sync.dma_start(list1[:], offs)
+        nc.sync.dma_start(list2[:], offs2)
+        nc.sync.dma_start(list3[:], offs3)
+        nc.sync.dma_start(out=share[:], in_=share2)
+        nc.sync.dma_start(out=old_sb[:], in_=old)
+        nc.vector.memset(f1[:], 0.0)
+        nc.vector.memset(f2[:], 0.0)
+
+        def quantise(raw, tag):
+            grouped = sb.tile([P, Q, PACK], BF16, name="grouped" + tag, align_bytes=64)
+            codes = sb.tile([P, Q], U32, name="codes" + tag, align_bytes=64)
+            scales = sb.tile([P, Q], U8, name="scales" + tag, align_bytes=64)
+            nc.vector.tensor_copy(
+                out=grouped[:].rearrange("p (c i) t -> p c t i", i=4),
+                in_=raw[:].rearrange("p t (c i) -> p c t i", i=4),
+            )
+            nc.vector.quantize_mx(out=codes[:].bitcast(FP8X4), scales=scales[:], in_=grouped[:].rearrange("p q t -> p (q t)"))
+            return codes, scales
+
+        def scores(codes, scales, tag, evacuate):
+            whole = sb.tile([P, T], F32, name="scores" + tag)
+            for c in range(T // N):
+                bank = psum.tile([P, N], F32, name="bank%s%d" % (tag, c))
+                nc.tensor.matmul_mx(
+                    out=bank[:],
+                    lhsT=codes[:].bitcast(FP8X4),
+                    lhsT_scale=scales[:],
+                    rhs=key_words[:, 2 * c * N : 2 * (c + 1) * N].bitcast(FP4X4),
+                    rhs_scale=key_scales[:, c * N : (c + 1) * N],
+                    start=True,
+                    stop=True,
+                )
+                evacuate(whole[:, c * N : (c + 1) * N], bank[:])
+            return whole
+
+        codes1, scales1 = quantise(raw1, "a")
+        a = scores(codes1, scales1, "a", lambda dst, src: nc.scalar.activation(dst, src, ACT.Copy))
+        codes2, scales2 = quantise(raw2, "b")
+        b = scores(codes2, scales2, "b", lambda dst, src: nc.vector.tensor_copy(dst, src))
+
+        picked = sb.tile([P, I], F32, name="picked")
+        s = sb.tile([P, I], F32, name="s")
+        for h in range(2):
+            slots = slice(h * HALF, (h + 1) * HALF)
+            cols = slice(h * HALF // 16, (h + 1) * HALF // 16)
+            nc.scalar.activation(picked[:, slots], a[:].indirect(list1[:, cols]), ACT.Copy)
+            nc.vector.tensor_tensor(s[:, slots], b[:].indirect(list2[:, cols]), picked[:, slots], ALU.mult)
+
+        neg_max = sb.tile([P, 1], F32, name="neg_max")
+        row_sum = sb.tile([P, 1], F32, name="row_sum")
+        inv_sum = sb.tile([P, 1], F32, name="inv_sum")
+        p = sb.tile([P, I], F32, name="p")
+        ws = sb.tile([P, I], F32, name="ws")
+        nc.vector.tensor_reduce(neg_max[:], s[:], mybir.AxisListType.X, ALU.max, negate=True)
+        nc.scalar.activation(p[:], s[:], ACT.Exp, bias=neg_max[:], accum_out=row_sum[:])
+        nc.vector.reciprocal(inv_sum[:], row_sum[:])
+        nc.vector.tensor_scalar(ws[:], p[:], inv_sum[:], 256.0, ALU.mult, ALU.mult)
+
+        nc.vector.tensor_copy(f1[:].indirect(list1[:]), ws[:])
+        nc.vector.tensor_copy(f2[:].indirect(list3[:]), ws[:])
+
+        for c in range(T // OUT_CHUNK):
+            cols = slice(c * OUT_CHUNK, (c + 1) * OUT_CHUNK)
+            part = sb.tile([P, OUT_CHUNK], F32, name="part%d" % c)
+            total = sb.tile([P, OUT_CHUNK], F32, name="total%d" % c)
+            nc.gpsimd.tensor_tensor(part[:], old_sb[:, cols], f1[:, cols], ALU.add)
+            nc.vector.scalar_tensor_tensor(total[:], f2[:, cols], share[:], part[:], ALU.mult, ALU.add)
+            queue = nc.sync if c % 2 == 0 else nc.scalar
+            queue.dma_start(out=out[:, cols], in_=total[:])

@@ -41,11 +41,11 @@ def tile_attend_crossproduct_soft_twiceput_heads_kernel(tc, query, query2, keys_
         f1 = sb.tile([P, T], F32, name="f1")
         f2 = sb.tile([P, T], F32, name="f2")
 
-        nc.vector.memset(key_scales[:].bitcast(I32), 0)
         nc.sync.dma_start(out=raw1[:], in_=query.rearrange("(p j) q -> p j q", j=PACK))
         nc.sync.dma_start(out=key_words[:].bitcast(I32), in_=keys_words[0].bitcast(I32))
         for g in range(4):
-            nc.scalar.dma_start(out=key_scales[32 * g : 32 * g + 4, :].bitcast(I32), in_=keys_scales[0, 4 * g : 4 * g + 4, :].bitcast(I32))
+            queue = nc.scalar if g < 3 else nc.sync
+            queue.dma_start(out=key_scales[32 * g : 32 * g + 4, :].bitcast(I32), in_=keys_scales[0, 4 * g : 4 * g + 4, :].bitcast(I32))
         nc.sync.dma_start(out=raw2[:], in_=query2.rearrange("(p j) q -> p j q", j=PACK))
         nc.sync.dma_start(list1[:], offs)
         nc.sync.dma_start(list2[:], offs2)
@@ -59,11 +59,14 @@ def tile_attend_crossproduct_soft_twiceput_heads_kernel(tc, query, query2, keys_
             grouped = sb.tile([P, Q, PACK], BF16, name="grouped" + tag, align_bytes=64)
             codes = sb.tile([P, Q], U32, name="codes" + tag, align_bytes=64)
             scales = sb.tile([P, Q], U8, name="scales" + tag, align_bytes=64)
-            nc.vector.tensor_copy(
-                out=grouped[:].rearrange("p (c i) t -> p c t i", i=4),
-                in_=raw[:].rearrange("p t (c i) -> p c t i", i=4),
-            )
-            nc.vector.quantize_mx(out=codes[:].bitcast(FP8X4), scales=scales[:], in_=grouped[:].rearrange("p q t -> p (q t)"))
+            halves = [slice(h * Q // 2, (h + 1) * Q // 2) for h in range(2)]
+            for rows in halves:
+                nc.vector.tensor_copy(
+                    out=grouped[:, rows, :].rearrange("p (c i) t -> p c t i", i=4),
+                    in_=raw[:, :, rows].rearrange("p t (c i) -> p c t i", i=4),
+                )
+            for rows in halves:
+                nc.vector.quantize_mx(out=codes[:, rows].bitcast(FP8X4), scales=scales[:, rows], in_=grouped[:, rows, :].rearrange("p q t -> p (q t)"))
             return codes, scales
 
         def scores(codes, scales, tag, evacuate):

from contextlib import ExitStack

import concourse.mybir as mybir

D, T, I, Q = 512, 1024, 512, 128
FLOPS = 2 * 2 * D * Q * T

F32 = mybir.dt.float32
BF16 = mybir.dt.bfloat16
I32 = mybir.dt.int32
U32 = mybir.dt.uint32
U16 = mybir.dt.uint16
U8 = mybir.dt.uint8
FP8X4 = mybir.dt.float8_e4m3fn_x4
FP4X4 = mybir.dt.float4_e2m1fn_x4
ALU = mybir.AluOpType
ACT = mybir.ActivationFunctionType

P = 128
PACK = 4
N = 256
HALF = I // 2
OUT_CHUNK = 256


def tile_attend_crossproduct_soft_twiceput_heads_kernel(tc, query, query2, keys_words, keys_scales, old, share2, offs, offs2, offs3, out):
    nc = tc.nc
    with ExitStack() as ctx:
        sb = ctx.enter_context(tc.tile_pool(name="sb", bufs=1))
        psum = ctx.enter_context(tc.psum_pool(name="psum", bufs=1))

        list1 = sb.tile([P, I // 16], U16, name="list1")
        list2 = sb.tile([P, I // 16], U16, name="list2")
        list3 = sb.tile([P, I // 16], U16, name="list3")
        raw1 = sb.tile([P, PACK, Q], F32, name="raw1")
        raw2 = sb.tile([P, PACK, Q], F32, name="raw2")
        key_words = sb.tile([P, 2 * T], U8, name="key_words", align_bytes=64)
        key_scales = sb.tile([P, T], U8, name="key_scales", align_bytes=64)
        old_sb = sb.tile([P, T], F32, name="old_sb")
        share = sb.tile([P, 1], F32, name="share")
        f1 = sb.tile([P, T], F32, name="f1")
        f2 = sb.tile([P, T], F32, name="f2")

        nc.sync.dma_start(out=raw1[:], in_=query.rearrange("(p j) q -> p j q", j=PACK))
        nc.sync.dma_start(out=key_words[:].bitcast(I32), in_=keys_words[0].bitcast(I32))
        for g in range(4):
            queue = nc.scalar if g < 3 else nc.sync
            queue.dma_start(out=key_scales[32 * g : 32 * g + 4, :].bitcast(I32), in_=keys_scales[0, 4 * g : 4 * g + 4, :].bitcast(I32))
        nc.sync.dma_start(out=raw2[:], in_=query2.rearrange("(p j) q -> p j q", j=PACK))
        nc.sync.dma_start(list1[:], offs)
        nc.sync.dma_start(list2[:], offs2)
        nc.sync.dma_start(list3[:], offs3)
        nc.sync.dma_start(out=share[:], in_=share2)
        nc.sync.dma_start(out=old_sb[:], in_=old)
        nc.vector.memset(f1[:], 0.0)
        nc.vector.memset(f2[:], 0.0)

        def quantise(raw, tag):
            grouped = sb.tile([P, Q, PACK], BF16, name="grouped" + tag, align_bytes=64)
            codes = sb.tile([P, Q], U32, name="codes" + tag, align_bytes=64)
            scales = sb.tile([P, Q], U8, name="scales" + tag, align_bytes=64)
            halves = [slice(h * Q // 2, (h + 1) * Q // 2) for h in range(2)]
            for rows in halves:
                nc.vector.tensor_copy(
                    out=grouped[:, rows, :].rearrange("p (c i) t -> p c t i", i=4),
                    in_=raw[:, :, rows].rearrange("p t (c i) -> p c t i", i=4),
                )
            for rows in halves:
                nc.vector.quantize_mx(out=codes[:, rows].bitcast(FP8X4), scales=scales[:, rows], in_=grouped[:, rows, :].rearrange("p q t -> p (q t)"))
            return codes, scales

        def scores(codes, scales, tag, evacuate):
            whole = sb.tile([P, T], F32, name="scores" + tag)
            for c in range(T // N):
                bank = psum.tile([P, N], F32, name="bank%s%d" % (tag, c))
                nc.tensor.matmul_mx(
                    out=bank[:],
                    lhsT=codes[:].bitcast(FP8X4),
                    lhsT_scale=scales[:],
                    rhs=key_words[:, 2 * c * N : 2 * (c + 1) * N].bitcast(FP4X4),
                    rhs_scale=key_scales[:, c * N : (c + 1) * N],
                    start=True,
                    stop=True,
                )
                evacuate(whole[:, c * N : (c + 1) * N], bank[:])
            return whole

        codes1, scales1 = quantise(raw1, "a")
        a = scores(codes1, scales1, "a", lambda dst, src: nc.scalar.activation(dst, src, ACT.Copy))
        codes2, scales2 = quantise(raw2, "b")
        b = scores(codes2, scales2, "b", lambda dst, src: nc.vector.tensor_copy(dst, src))

        picked = sb.tile([P, I], F32, name="picked")
        s = sb.tile([P, I], F32, name="s")
        for h in range(2):
            slots = slice(h * HALF, (h + 1) * HALF)
            cols = slice(h * HALF // 16, (h + 1) * HALF // 16)
            nc.scalar.activation(picked[:, slots], a[:].indirect(list1[:, cols]), ACT.Copy)
            nc.vector.tensor_tensor(s[:, slots], b[:].indirect(list2[:, cols]), picked[:, slots], ALU.mult)

        neg_max = sb.tile([P, 1], F32, name="neg_max")
        row_sum = sb.tile([P, 1], F32, name="row_sum")
        inv_sum = sb.tile([P, 1], F32, name="inv_sum")
        p = sb.tile([P, I], F32, name="p")
        ws = sb.tile([P, I], F32, name="ws")
        nc.vector.tensor_reduce(neg_max[:], s[:], mybir.AxisListType.X, ALU.max, negate=True)
        nc.scalar.activation(p[:], s[:], ACT.Exp, bias=neg_max[:], accum_out=row_sum[:])
        nc.vector.reciprocal(inv_sum[:], row_sum[:])
        nc.vector.tensor_scalar(ws[:], p[:], inv_sum[:], 256.0, ALU.mult, ALU.mult)

        nc.vector.tensor_copy(f1[:].indirect(list1[:]), ws[:])
        nc.vector.tensor_copy(f2[:].indirect(list3[:]), ws[:])

        for c in range(T // OUT_CHUNK):
            cols = slice(c * OUT_CHUNK, (c + 1) * OUT_CHUNK)
            part = sb.tile([P, OUT_CHUNK], F32, name="part%d" % c)
            total = sb.tile([P, OUT_CHUNK], F32, name="total%d" % c)
            nc.gpsimd.tensor_tensor(part[:], old_sb[:, cols], f1[:, cols], ALU.add)
            nc.vector.scalar_tensor_tensor(total[:], f2[:, cols], share[:], part[:], ALU.mult, ALU.add)
            queue = nc.sync if c % 2 == 0 else nc.scalar
            queue.dma_start(out=out[:, cols], in_=total[:])
